import numpy as np
import ml_dtypes


def mxq(x, axis, fmt="e4m3"):
    dtype, down = {"e4m3": (ml_dtypes.float8_e4m3fn, 7), "e5m2": (ml_dtypes.float8_e5m2, 14)}[fmt]
    v = np.moveaxis(np.asarray(x, np.float32).astype(ml_dtypes.bfloat16).astype(np.float64), axis, -1)
    blocks = v.reshape(v.shape[:-1] + (-1, 32))
    amax = np.abs(blocks).max(-1, keepdims=True)
    byte = np.maximum(np.where(amax > 0, np.frexp(amax)[1] - 1 + 127, 0) - down, 1)
    scale = np.exp2(byte - 127.0)
    codes = (blocks / scale).astype(np.float32).astype(dtype).astype(np.float64)
    return np.moveaxis((codes * scale).reshape(v.shape), -1, axis)


WIDE = False


def mx_kscale(k):
    if not WIDE:
        return np.ones(k)
    levels = np.array([10, -10, 5, -5, 0])
    if k % 512:
        return np.exp2(np.random.permutation(np.resize(levels, k // 32))).repeat(32)
    a = np.empty((k // 512, 16))
    for p in range(k // 512):
        a[p, :8] = np.random.permutation(np.resize(levels, 8))
        for g in range(8):
            far = levels[np.abs(levels - a[p, g]) >= 10]
            a[p, g + 8] = far[np.random.randint(len(far))]
    return np.exp2(a.ravel()).repeat(32)


def f64(x):
    return np.asarray(x).astype(np.float64)


def striped(idx):
    return np.tile(np.asarray(idx).reshape(-1, 16).T, (8, 1)).astype(np.uint16)


def unstriped(offs):
    return offs[:16].T.reshape(-1).astype(np.int64)


B, N, C, D, NQ = 1, 256, 4096, 1024, 256


def eight(codes):
    return np.concatenate([codes[h].reshape(-1, 16).T for h in range(8)]).astype(np.uint16)


def uneight(offs):
    return np.stack([offs[16 * h:16 * h + 16].T.reshape(-1) for h in range(8)]).astype(np.int64)


def setup_inputs():
    n = np.random.standard_normal
    s = mx_kscale(D)[:, None]
    grid = lambda x: np.round(x * 32) / 32
    return {
        "qT": (n((B, D, NQ)) * s / np.sqrt(D)).astype(np.float32),
        "cb": (grid(n((D, C))) / s).astype(np.float32),
        "norm": np.tile(np.random.randint(32, 129, N) / 64.0, (128, 1)).astype(np.float32),
        "offs": eight(np.random.randint(0, C, (8, N))),
        "offs2": eight(np.random.randint(0, C, (8, N))),
    }


def reference(qT, cb, norm, offs, offs2):
    k = []
    for part, offs_ in enumerate((offs, offs2,)):
        codes = uneight(offs_)
        k += [f64(cb)[512 * part + 64 * h:512 * part + 64 * h + 64][:, codes[h]] for h in range(8)]
    k = np.concatenate(k) * f64(norm)[:1]
    a = mxq(f64(qT), 1, "e4m3").transpose(0, 2, 1) @ mxq(k, 0, "e4m3")
    return a

@@ -1,0 +1,106 @@
+import concourse.mybir as mybir
+
+FLOPS = 2 * 256 * 256 * 1024
+
+F32 = mybir.dt.float32
+BF16 = mybir.dt.bfloat16
+U32 = mybir.dt.uint32
+U16 = mybir.dt.uint16
+U8 = mybir.dt.uint8
+FP8X4 = mybir.dt.float8_e4m3fn_x4
+MULT = mybir.AluOpType.mult
+
+P = 128
+PARTS = 2
+ROWS = 4
+CODEWORDS = 4096
+NQ = 256
+N = 256
+HALF = 128
+M_TILE = 128
+
+
+def tile_attend_pq_att_kernel(tc, qT, cb, norm, offs, offs2, out):
+    nc = tc.nc
+    rows = cb.rearrange("(g p t) c -> g t p c", g=PARTS, p=P, t=ROWS)
+    halves = [slice(h * HALF, (h + 1) * HALF) for h in range(N // HALF)]
+    m_tiles = [slice(m * M_TILE, (m + 1) * M_TILE) for m in range(NQ // M_TILE)]
+
+    with (
+        tc.tile_pool(name="keep", bufs=1) as keep,
+        tc.tile_pool(name="picked", bufs=3) as picked_pool,
+        tc.psum_pool(name="psum", bufs=1) as psum,
+    ):
+        offsets = keep.tile([P, N // 16], U16, name="offsets")
+        offsets2 = keep.tile([P, N // 16], U16, name="offsets2")
+        scale = keep.tile([P, N], F32, name="scale")
+        q_raw = keep.tile([P, PARTS, ROWS * NQ], F32, name="q_raw")
+        books = [
+            [keep.tile([P, CODEWORDS], F32, name=f"book_{g}_{t}") for t in range(ROWS)]
+            for g in range(PARTS)
+        ]
+
+        nc.sync.dma_start(books[0][0][:], rows[0, 0])
+        nc.sync.dma_start(offsets[:], offs)
+        nc.sync.dma_start(offsets2[:], offs2)
+        nc.sync.dma_start(scale[:], norm)
+        nc.sync.dma_start(books[0][1][:], rows[0, 1])
+        nc.sync.dma_start(q_raw[:], qT[0].rearrange("(g p t) q -> p g (t q)", g=PARTS, t=ROWS))
+        for g in range(PARTS):
+            for t in range(ROWS):
+                if (g, t) > (0, 1):
+                    nc.sync.dma_start(books[g][t][:], rows[g, t])
+
+        q_bf = keep.tile([P, PARTS, NQ, ROWS], BF16, name="q_bf", align_bytes=64)
+        q_codes = keep.tile([P, PARTS * NQ], U32, name="q_codes", align_bytes=64)
+        q_scales = keep.tile([P, PARTS * NQ], U8, name="q_scales", align_bytes=64)
+        for g in range(PARTS):
+            nc.scalar.copy(q_bf[:, g], q_raw[:, g].rearrange("p (t q) -> p q t", t=ROWS))
+        nc.vector.quantize_mx(
+            out=q_codes[:].bitcast(FP8X4),
+            scales=q_scales[:],
+            in_=q_bf[:].rearrange("p g q t -> p (g q t)"),
+        )
+
+        sums = [
+            [psum.tile([M_TILE, HALF], F32, name=f"sums_{m}_{h}") for h in range(len(halves))]
+            for m in range(len(m_tiles))
+        ]
+        for g, lists in enumerate((offsets, offsets2)):
+            k_bf = keep.tile([P, N, ROWS], BF16, name=f"k_bf_{g}", align_bytes=64)
+            k_codes = keep.tile([P, N], U32, name=f"k_codes_{g}", align_bytes=64)
+            k_scales = keep.tile([P, N], U8, name=f"k_scales_{g}", align_bytes=64)
+            for t in range(ROWS):
+                picked = picked_pool.tile([P, N], F32, name="picked", align_bytes=64)
+                for h, cols in enumerate(halves):
+                    codes = lists[:, h * HALF // 16 : (h + 1) * HALF // 16]
+                    nc.vector.tensor_tensor(
+                        picked[:, cols], books[g][t][:].indirect(codes), scale[:, cols], MULT
+                    )
+                for cols in halves:
+                    nc.vector.tensor_copy(k_bf[:, cols, t], picked[:, cols])
+            for cols in halves:
+                nc.vector.quantize_mx(
+                    out=k_codes[:, cols].bitcast(FP8X4),
+                    scales=k_scales[:, cols],
+                    in_=k_bf[:, cols, :].rearrange("p n t -> p (n t)"),
+                )
+            for h, cols in enumerate(halves):
+                for m in range(len(m_tiles)):
+                    q_cols = slice(g * NQ + m * M_TILE, g * NQ + (m + 1) * M_TILE)
+                    nc.tensor.matmul_mx(
+                        out=sums[m][h][:],
+                        lhsT=q_codes[:, q_cols].bitcast(FP8X4),
+                        lhsT_scale=q_scales[:, q_cols],
+                        rhs=k_codes[:, cols].bitcast(FP8X4),
+                        rhs_scale=k_scales[:, cols],
+                        start=(g == 0),
+                        stop=(g == PARTS - 1),
+                    )
+
+        results = [keep.tile([M_TILE, N], F32, name=f"result_{m}") for m in range(len(m_tiles))]
+        for h, cols in enumerate(halves):
+            nc.vector.tensor_copy(results[0][:, cols], sums[0][h][:])
+            nc.scalar.copy(results[1][:, cols], sums[1][h][:])
+        nc.sync.dma_start(out[0, m_tiles[0], :], results[0][:])
+        nc.scalar.dma_start(out[0, m_tiles[1], :], results[1][:])

@@ -23,18 +23,18 @@ M_TILE = 128
 def tile_attend_pq_att_kernel(tc, qT, cb, norm, offs, offs2, out):
     nc = tc.nc
     rows = cb.rearrange("(g p t) c -> g t p c", g=PARTS, p=P, t=ROWS)
+    q_rows = qT[0].rearrange("(g p t) q -> g p t q", g=PARTS, t=ROWS)
     halves = [slice(h * HALF, (h + 1) * HALF) for h in range(N // HALF)]
     m_tiles = [slice(m * M_TILE, (m + 1) * M_TILE) for m in range(NQ // M_TILE)]
 
     with (
         tc.tile_pool(name="keep", bufs=1) as keep,
-        tc.tile_pool(name="picked", bufs=3) as picked_pool,
         tc.psum_pool(name="psum", bufs=1) as psum,
     ):
         offsets = keep.tile([P, N // 16], U16, name="offsets")
         offsets2 = keep.tile([P, N // 16], U16, name="offsets2")
         scale = keep.tile([P, N], F32, name="scale")
-        q_raw = keep.tile([P, PARTS, ROWS * NQ], F32, name="q_raw")
+        q_raw = [keep.tile([P, ROWS, NQ], F32, name=f"q_raw_{g}") for g in range(PARTS)]
         books = [
             [keep.tile([P, CODEWORDS], F32, name=f"book_{g}_{t}") for t in range(ROWS)]
             for g in range(PARTS)
@@ -43,64 +43,60 @@ def tile_attend_pq_att_kernel(tc, qT, cb, norm, offs, offs2, out):
         nc.sync.dma_start(books[0][0][:], rows[0, 0])
         nc.sync.dma_start(offsets[:], offs)
         nc.sync.dma_start(offsets2[:], offs2)
-        nc.sync.dma_start(scale[:], norm)
-        nc.sync.dma_start(books[0][1][:], rows[0, 1])
-        nc.sync.dma_start(q_raw[:], qT[0].rearrange("(g p t) q -> p g (t q)", g=PARTS, t=ROWS))
+        nc.scalar.dma_start(scale[:], norm)
         for g in range(PARTS):
             for t in range(ROWS):
-                if (g, t) > (0, 1):
+                if (g, t) > (0, 0):
                     nc.sync.dma_start(books[g][t][:], rows[g, t])
-
-        q_bf = keep.tile([P, PARTS, NQ, ROWS], BF16, name="q_bf", align_bytes=64)
-        q_codes = keep.tile([P, PARTS * NQ], U32, name="q_codes", align_bytes=64)
-        q_scales = keep.tile([P, PARTS * NQ], U8, name="q_scales", align_bytes=64)
         for g in range(PARTS):
-            nc.scalar.copy(q_bf[:, g], q_raw[:, g].rearrange("p (t q) -> p q t", t=ROWS))
-        nc.vector.quantize_mx(
-            out=q_codes[:].bitcast(FP8X4),
-            scales=q_scales[:],
-            in_=q_bf[:].rearrange("p g q t -> p (g q t)"),
-        )
+            nc.sync.dma_start(q_raw[g][:], q_rows[g])
 
-        sums = [
-            [psum.tile([M_TILE, HALF], F32, name=f"sums_{m}_{h}") for h in range(len(halves))]
-            for m in range(len(m_tiles))
-        ]
+        k_codes = [keep.tile([P, N], U32, name=f"k_codes_{g}", align_bytes=64) for g in range(PARTS)]
+        k_scales = [keep.tile([P, N], U8, name=f"k_scales_{g}", align_bytes=64) for g in range(PARTS)]
         for g, lists in enumerate((offsets, offsets2)):
-            k_bf = keep.tile([P, N, ROWS], BF16, name=f"k_bf_{g}", align_bytes=64)
-            k_codes = keep.tile([P, N], U32, name=f"k_codes_{g}", align_bytes=64)
-            k_scales = keep.tile([P, N], U8, name=f"k_scales_{g}", align_bytes=64)
+            picked = [keep.tile([P, ROWS, HALF], F32, name=f"picked_{g}_{h}") for h in range(len(halves))]
+            k_bf = [keep.tile([P, HALF, ROWS], BF16, name=f"k_bf_{g}_{h}", align_bytes=64) for h in range(len(halves))]
             for t in range(ROWS):
-                picked = picked_pool.tile([P, N], F32, name="picked", align_bytes=64)
                 for h, cols in enumerate(halves):
                     codes = lists[:, h * HALF // 16 : (h + 1) * HALF // 16]
                     nc.vector.tensor_tensor(
-                        picked[:, cols], books[g][t][:].indirect(codes), scale[:, cols], MULT
+                        picked[h][:, t, :], books[g][t][:].indirect(codes), scale[:, cols], MULT
                     )
-                for cols in halves:
-                    nc.vector.tensor_copy(k_bf[:, cols, t], picked[:, cols])
-            for cols in halves:
-                nc.vector.quantize_mx(
-                    out=k_codes[:, cols].bitcast(FP8X4),
-                    scales=k_scales[:, cols],
-                    in_=k_bf[:, cols, :].rearrange("p n t -> p (n t)"),
-                )
+            nc.scalar.copy(k_bf[0][:], picked[0][:].rearrange("p t n -> p n t"))
+            nc.vector.tensor_copy(k_bf[1][:], picked[1][:].rearrange("p t n -> p n t"))
             for h, cols in enumerate(halves):
-                for m in range(len(m_tiles)):
-                    q_cols = slice(g * NQ + m * M_TILE, g * NQ + (m + 1) * M_TILE)
-                    nc.tensor.matmul_mx(
-                        out=sums[m][h][:],
-                        lhsT=q_codes[:, q_cols].bitcast(FP8X4),
-                        lhsT_scale=q_scales[:, q_cols],
-                        rhs=k_codes[:, cols].bitcast(FP8X4),
-                        rhs_scale=k_scales[:, cols],
-                        start=(g == 0),
-                        stop=(g == PARTS - 1),
-                    )
+                nc.vector.quantize_mx(
+                    out=k_codes[g][:, cols].bitcast(FP8X4),
+                    scales=k_scales[g][:, cols],
+                    in_=k_bf[h][:].rearrange("p n t -> p (n t)"),
+                )
+
+        sums = [psum.tile([M_TILE, N], F32, name=f"sums_{m}") for m in range(len(m_tiles))]
+        for g in range(PARTS):
+            q_bf = [keep.tile([P, M_TILE, ROWS], BF16, name=f"q_bf_{g}_{m}", align_bytes=64) for m in range(len(m_tiles))]
+            q_codes = [keep.tile([P, M_TILE], U32, name=f"q_codes_{g}_{m}", align_bytes=64) for m in range(len(m_tiles))]
+            q_scales = [keep.tile([P, M_TILE], U8, name=f"q_scales_{g}_{m}", align_bytes=64) for m in range(len(m_tiles))]
+            nc.scalar.copy(q_bf[0][:], q_raw[g][:, :, m_tiles[0]].rearrange("p t q -> p q t"))
+            nc.vector.tensor_copy(q_bf[1][:], q_raw[g][:, :, m_tiles[1]].rearrange("p t q -> p q t"))
+            for m in reversed(range(len(m_tiles))):
+                nc.vector.quantize_mx(
+                    out=q_codes[m][:].bitcast(FP8X4),
+                    scales=q_scales[m][:],
+                    in_=q_bf[m][:].rearrange("p q t -> p (q t)"),
+                )
+            for m in reversed(range(len(m_tiles))):
+                nc.tensor.matmul_mx(
+                    out=sums[m][:],
+                    lhsT=q_codes[m][:].bitcast(FP8X4),
+                    lhsT_scale=q_scales[m][:],
+                    rhs=k_codes[g][:].bitcast(FP8X4),
+                    rhs_scale=k_scales[g][:],
+                    start=(g == 0),
+                    stop=(g == PARTS - 1),
+                )
 
         results = [keep.tile([M_TILE, N], F32, name=f"result_{m}") for m in range(len(m_tiles))]
-        for h, cols in enumerate(halves):
-            nc.vector.tensor_copy(results[0][:, cols], sums[0][h][:])
-            nc.scalar.copy(results[1][:, cols], sums[1][h][:])
-        nc.sync.dma_start(out[0, m_tiles[0], :], results[0][:])
-        nc.scalar.dma_start(out[0, m_tiles[1], :], results[1][:])
+        nc.vector.tensor_copy(results[1][:], sums[1][:])
+        nc.sync.dma_start(out[0, m_tiles[1], :], results[1][:])
+        nc.scalar.copy(results[0][:], sums[0][:])
+        nc.scalar.dma_start(out[0, m_tiles[0], :], results[0][:])

import concourse.mybir as mybir

FLOPS = 2 * 256 * 256 * 1024

F32 = mybir.dt.float32
BF16 = mybir.dt.bfloat16
U32 = mybir.dt.uint32
U16 = mybir.dt.uint16
U8 = mybir.dt.uint8
FP8X4 = mybir.dt.float8_e4m3fn_x4
MULT = mybir.AluOpType.mult

P = 128
PARTS = 2
ROWS = 4
CODEWORDS = 4096
NQ = 256
N = 256
HALF = 128
M_TILE = 128


def tile_attend_pq_att_kernel(tc, qT, cb, norm, offs, offs2, out):
    nc = tc.nc
    rows = cb.rearrange("(g p t) c -> g t p c", g=PARTS, p=P, t=ROWS)
    q_rows = qT[0].rearrange("(g p t) q -> g p t q", g=PARTS, t=ROWS)
    halves = [slice(h * HALF, (h + 1) * HALF) for h in range(N // HALF)]
    m_tiles = [slice(m * M_TILE, (m + 1) * M_TILE) for m in range(NQ // M_TILE)]

    with (
        tc.tile_pool(name="keep", bufs=1) as keep,
        tc.psum_pool(name="psum", bufs=1) as psum,
    ):
        offsets = keep.tile([P, N // 16], U16, name="offsets")
        offsets2 = keep.tile([P, N // 16], U16, name="offsets2")
        scale = keep.tile([P, N], F32, name="scale")
        q_raw = [keep.tile([P, ROWS, NQ], F32, name=f"q_raw_{g}") for g in range(PARTS)]
        books = [
            [keep.tile([P, CODEWORDS], F32, name=f"book_{g}_{t}") for t in range(ROWS)]
            for g in range(PARTS)
        ]

        nc.sync.dma_start(books[0][0][:], rows[0, 0])
        nc.sync.dma_start(offsets[:], offs)
        nc.sync.dma_start(offsets2[:], offs2)
        nc.scalar.dma_start(scale[:], norm)
        for g in range(PARTS):
            for t in range(ROWS):
                if (g, t) > (0, 0):
                    nc.sync.dma_start(books[g][t][:], rows[g, t])
        for g in range(PARTS):
            nc.sync.dma_start(q_raw[g][:], q_rows[g])

        k_codes = [keep.tile([P, N], U32, name=f"k_codes_{g}", align_bytes=64) for g in range(PARTS)]
        k_scales = [keep.tile([P, N], U8, name=f"k_scales_{g}", align_bytes=64) for g in range(PARTS)]
        for g, lists in enumerate((offsets, offsets2)):
            picked = [keep.tile([P, ROWS, HALF], F32, name=f"picked_{g}_{h}") for h in range(len(halves))]
            k_bf = [keep.tile([P, HALF, ROWS], BF16, name=f"k_bf_{g}_{h}", align_bytes=64) for h in range(len(halves))]
            for t in range(ROWS):
                for h, cols in enumerate(halves):
                    codes = lists[:, h * HALF // 16 : (h + 1) * HALF // 16]
                    nc.vector.tensor_tensor(
                        picked[h][:, t, :], books[g][t][:].indirect(codes), scale[:, cols], MULT
                    )
            nc.scalar.copy(k_bf[0][:], picked[0][:].rearrange("p t n -> p n t"))
            nc.vector.tensor_copy(k_bf[1][:], picked[1][:].rearrange("p t n -> p n t"))
            for h, cols in enumerate(halves):
                nc.vector.quantize_mx(
                    out=k_codes[g][:, cols].bitcast(FP8X4),
                    scales=k_scales[g][:, cols],
                    in_=k_bf[h][:].rearrange("p n t -> p (n t)"),
                )

        sums = [psum.tile([M_TILE, N], F32, name=f"sums_{m}") for m in range(len(m_tiles))]
        for g in range(PARTS):
            q_bf = [keep.tile([P, M_TILE, ROWS], BF16, name=f"q_bf_{g}_{m}", align_bytes=64) for m in range(len(m_tiles))]
            q_codes = [keep.tile([P, M_TILE], U32, name=f"q_codes_{g}_{m}", align_bytes=64) for m in range(len(m_tiles))]
            q_scales = [keep.tile([P, M_TILE], U8, name=f"q_scales_{g}_{m}", align_bytes=64) for m in range(len(m_tiles))]
            nc.scalar.copy(q_bf[0][:], q_raw[g][:, :, m_tiles[0]].rearrange("p t q -> p q t"))
            nc.vector.tensor_copy(q_bf[1][:], q_raw[g][:, :, m_tiles[1]].rearrange("p t q -> p q t"))
            for m in reversed(range(len(m_tiles))):
                nc.vector.quantize_mx(
                    out=q_codes[m][:].bitcast(FP8X4),
                    scales=q_scales[m][:],
                    in_=q_bf[m][:].rearrange("p q t -> p (q t)"),
                )
            for m in reversed(range(len(m_tiles))):
                nc.tensor.matmul_mx(
                    out=sums[m][:],
                    lhsT=q_codes[m][:].bitcast(FP8X4),
                    lhsT_scale=q_scales[m][:],
                    rhs=k_codes[g][:].bitcast(FP8X4),
                    rhs_scale=k_scales[g][:],
                    start=(g == 0),
                    stop=(g == PARTS - 1),
                )

        results = [keep.tile([M_TILE, N], F32, name=f"result_{m}") for m in range(len(m_tiles))]
        nc.vector.tensor_copy(results[1][:], sums[1][:])
        nc.sync.dma_start(out[0, m_tiles[1], :], results[1][:])
        nc.scalar.copy(results[0][:], sums[0][:])
        nc.scalar.dma_start(out[0, m_tiles[0], :], results[0][:])
